import numpy as np
import ml_dtypes


def mxq(x, axis, fmt="e4m3"):
    dtype, down = {"e4m3": (ml_dtypes.float8_e4m3fn, 7), "e5m2": (ml_dtypes.float8_e5m2, 14)}[fmt]
    v = np.moveaxis(np.asarray(x, np.float32).astype(ml_dtypes.bfloat16).astype(np.float64), axis, -1)
    blocks = v.reshape(v.shape[:-1] + (-1, 32))
    amax = np.abs(blocks).max(-1, keepdims=True)
    byte = np.maximum(np.where(amax > 0, np.frexp(amax)[1] - 1 + 127, 0) - down, 1)
    scale = np.exp2(byte - 127.0)
    codes = (blocks / scale).astype(np.float32).astype(dtype).astype(np.float64)
    return np.moveaxis((codes * scale).reshape(v.shape), -1, axis)


WIDE = False


def mx_kscale(k):
    if not WIDE:
        return np.ones(k)
    levels = np.array([10, -10, 5, -5, 0])
    if k % 512:
        return np.exp2(np.random.permutation(np.resize(levels, k // 32))).repeat(32)
    a = np.empty((k // 512, 16))
    for p in range(k // 512):
        a[p, :8] = np.random.permutation(np.resize(levels, 8))
        for g in range(8):
            far = levels[np.abs(levels - a[p, g]) >= 10]
            a[p, g + 8] = far[np.random.randint(len(far))]
    return np.exp2(a.ravel()).repeat(32)


def f64(x):
    return np.asarray(x).astype(np.float64)


def striped(idx):
    return np.tile(np.asarray(idx).reshape(-1, 16).T, (8, 1)).astype(np.uint16)


def unstriped(offs):
    return offs[:16].T.reshape(-1).astype(np.int64)


E2M1 = np.array([0.0, 0.5, 1.0, 1.5, 2.0, 3.0, 4.0, 6.0, -0.0, -0.5, -1.0, -1.5, -2.0, -3.0, -4.0, -6.0])


def pack_weight(w, fmt):
    k, n = w.shape
    w = f64(np.asarray(w, np.float32).astype(ml_dtypes.bfloat16)).reshape(k // 32, 32, n)
    amax = np.abs(w).max(1)
    if fmt == "e4m3":
        byte = np.frexp(amax)[1] - 1 + 127 - 7
    else:
        mant, ex = np.frexp(amax / 6.0)
        byte = np.where(mant > 0.5, ex, ex - 1) + 127
    byte = np.clip(np.where(amax > 0, byte, 1), 1, 254)
    scaled = (w * np.exp2(127.0 - byte)[:, None, :]).reshape(k, n).astype(np.float32)
    by_word = np.ascontiguousarray(scaled.reshape(k // 512, 128, 4, n).transpose(0, 1, 3, 2))
    if fmt == "e4m3":
        words = by_word.astype(ml_dtypes.float8_e4m3fn).view(np.uint8)
    else:
        c = by_word.astype(ml_dtypes.float4_e2m1fn).view(np.uint8) & 0xF
        words = (c[..., 0::2] | (c[..., 1::2] << 4)).reshape(k // 512, 128, 2 * n)
    return np.ascontiguousarray(words), np.ascontiguousarray(byte.astype(np.uint8).reshape(k // 512, 16, n))


def unpack_weight(words, scales, fmt):
    g, _, n = scales.shape
    words = np.ascontiguousarray(words).reshape(g, 128, n, -1)
    if fmt == "e4m3":
        vals = words.view(ml_dtypes.float8_e4m3fn).astype(np.float64)
    else:
        nib = np.empty((g, 128, n, 4), np.uint8)
        nib[..., 0::2] = words & 0xF
        nib[..., 1::2] = words >> 4
        vals = E2M1[nib]
    vals = vals * np.repeat(np.exp2(scales.astype(np.float64) - 127.0), 8, axis=1)[..., None]
    return vals.transpose(0, 1, 3, 2).reshape(g * 512, n)


K, T, J, R, N = 1024, 1024, 512, 512, 512


def setup_inputs():
    n = np.random.standard_normal
    idx = np.random.permutation(T)[:J]
    fk = mx_kscale(K)
    fr = mx_kscale(R)
    xtp = pack_weight(n((K, T)) / fk[:, None], "e4m3")
    wap = pack_weight(n((K, R)) * np.random.uniform(0.3, 2.0, (1, R)) / np.sqrt(K) * fk[:, None], "e2m1")
    wbp = pack_weight(n((R, N)) * 1 / np.sqrt(R) / fr[:, None], "e4m3")
    return {
        "xt_words": xtp[0],
        "xt_scales": xtp[1],
        "wa_words": wap[0],
        "wa_scales": wap[1],
        "us": (np.random.uniform(0.5, 2.0, (R, 1)) * fr[:, None]).astype(np.float32),
        "wb_words": wbp[0],
        "wb_scales": wbp[1],
        "res": (1.0 * n((N, T))).astype(np.float32),
        "offs": striped(idx),
    }


def reference(xt_words, xt_scales, wa_words, wa_scales, us, wb_words, wb_scales, res, offs):
    idx = unstriped(offs)
    xtu = unpack_weight(xt_words, xt_scales, "e4m3")
    wau = unpack_weight(wa_words, wa_scales, "e2m1")
    wbu = unpack_weight(wb_words, wb_scales, "e4m3")
    xtidxg = xtu[:, idx]
    z = wau.T @ xtidxg
    hid = z / (np.max(np.abs(z), axis=1, keepdims=True) + 0.1) * f64(us)
    hidq = mxq(hid, 0, "e4m3")
    p = wbu.T @ hidq
    pp = np.zeros((N, T))
    pp[:, idx] = p
    y = pp + 0.2 * f64(res)
    return y

@@ -1,0 +1,235 @@
+from contextlib import ExitStack
+
+import concourse.mybir as mybir
+
+K, T, J, R, N = 1024, 1024, 512, 512, 512
+FLOPS = 2 * K * R * J + 2 * R * N * J
+
+F32 = mybir.dt.float32
+BF16 = mybir.dt.bfloat16
+I32 = mybir.dt.int32
+U32 = mybir.dt.uint32
+U16 = mybir.dt.uint16
+U8 = mybir.dt.uint8
+FP8X4 = mybir.dt.float8_e4m3fn_x4
+FP4X4 = mybir.dt.float4_e2m1fn_x4
+ALU = mybir.AluOpType
+ACT = mybir.ActivationFunctionType
+AXIS = mybir.AxisListType
+
+P = 128
+PACK = 4
+PASSES = K // (P * PACK)
+CHUNK = 128
+CHUNKS = J // CHUNK
+LANES = 16
+QUAD = 32
+ROWS = 4
+HALF = J // 2
+
+
+def tile_moe_expert_hidden_over_peak_kernel(
+    tc, xt_words, xt_scales, wa_words, wa_scales, us, wb_words, wb_scales, res, offs, out
+):
+    nc = tc.nc
+    with ExitStack() as ctx:
+        keep = ctx.enter_context(tc.tile_pool(name="keep", bufs=1))
+        reuse = ctx.enter_context(tc.tile_pool(name="reuse", bufs=1))
+        stage = ctx.enter_context(tc.tile_pool(name="stage", bufs=5))
+        zpsum = ctx.enter_context(tc.psum_pool(name="zpsum", bufs=1))
+        ppsum = ctx.enter_context(tc.psum_pool(name="ppsum", bufs=4))
+
+        def entries(first, count):
+            return offsets[:, first // LANES : (first + count) // LANES]
+
+        def load_scale_rows(queue, plane, scales):
+            rows = scales.bitcast(I32).rearrange("z (q i) c -> i q z c", i=ROWS)
+            for i in range(ROWS):
+                queue.dma_start(out=plane[i:P:QUAD].bitcast(I32), in_=rows[i])
+
+        offsets = keep.tile([P, J // LANES], U16, name="offsets")
+        x_scale = keep.tile([P, T], U8, name="x_scale", align_bytes=64)
+        wa_scale_raw = reuse.tile([P, PASSES, R], U8, name="wa_scale_raw", align_bytes=64, offset=0)
+        wb_scale = keep.tile([P, 1, N], U8, name="wb_scale", align_bytes=64)
+        xg_scale = [keep.tile([P, J], U8, name="xg_scale%d" % z, align_bytes=64) for z in range(PASSES)]
+        for plane in (x_scale, wa_scale_raw, xg_scale[1], wb_scale):
+            nc.vector.memset(plane[:].bitcast(I32), 0)
+
+        nc.sync.dma_start(offsets[:], offs)
+        for q in range(P // QUAD):
+            nc.sync.dma_start(
+                out=x_scale[QUAD * q : QUAD * q + PASSES * ROWS, :].bitcast(I32),
+                in_=xt_scales[:, ROWS * q : ROWS * (q + 1), :].bitcast(I32),
+            )
+        wa_raw = keep.tile([P, PASSES, 2 * R], U8, name="wa_raw", align_bytes=64)
+        nc.sync.dma_start(out=wa_raw[:].bitcast(I32), in_=wa_words.bitcast(I32).rearrange("z p c -> p z c"))
+        x_word = []
+        for z in range(PASSES):
+            x_word.append(keep.tile([P, T], U32, name="x_word%d" % z, align_bytes=64))
+            nc.sync.dma_start(
+                out=x_word[z][:].bitcast(I32),
+                in_=xt_words[z].rearrange("p c r -> p (c r)").bitcast(I32),
+            )
+        load_scale_rows(nc.scalar, wa_scale_raw, wa_scales)
+
+        nc.vector.tensor_copy(out=xg_scale[0][:], in_=x_scale[:].indirect(offsets[:]))
+        nc.scalar.dma_start(out=xg_scale[1][0:112, :].bitcast(I32), in_=xg_scale[0][ROWS : 112 + ROWS, :].bitcast(I32))
+
+        factor = keep.tile([P, PACK], F32, name="factor")
+        nc.sync.dma_start(out=factor[:], in_=us.rearrange("(p t) o -> p (t o)", t=PACK))
+        wb = keep.tile([P, N], U32, name="wb", align_bytes=64)
+        nc.sync.dma_start(out=wb[:].bitcast(I32), in_=wb_words[0].rearrange("p c r -> p (c r)").bitcast(I32))
+        load_scale_rows(nc.sync, wb_scale, wb_scales)
+        stream = []
+        for n in range(N // P):
+            stream.append(keep.tile([P, T], F32, name="stream%d" % n))
+            nc.sync.dma_start(out=stream[n][:], in_=res[n * P : (n + 1) * P, :])
+
+        placed = []
+        for b in range(3):
+            placed.append(keep.tile([P, T], F32, name="placed%d" % b))
+            nc.vector.memset(placed[b][:].bitcast(I32), 0)
+
+        xg_word = [
+            keep.tile([P, PASSES, HALF], U32, name="xg_word0", align_bytes=64),
+            reuse.tile([P, PASSES, HALF], U32, name="xg_word1", align_bytes=64, offset=0),
+        ]
+        wa = keep.tile([P, PASSES, 2 * R], U8, name="wa", align_bytes=64)
+        wa_scale = keep.tile([P, PASSES, R], U8, name="wa_scale", align_bytes=64)
+        nc.vector.tensor_copy(
+            out=wa[:].bitcast(U16).rearrange("p z (t h l) -> p z h t l", t=PACK, l=8),
+            in_=wa_raw[:].bitcast(U16).rearrange("p z (h l t) -> p z h t l", t=PACK, l=8),
+        )
+        nc.vector.tensor_copy(
+            out=wa_scale[:].rearrange("p z (t h l) -> p z h t l", t=PACK, l=16),
+            in_=wa_scale_raw[:].rearrange("p z (h l t) -> p z h t l", t=PACK, l=16),
+        )
+
+        z_bank = [zpsum.tile([P, PACK, CHUNK], F32, name="z_bank%d" % c) for c in range(CHUNKS)]
+        last = CHUNKS - 1
+        size = [keep.tile([P, PACK, CHUNK], F32, name="size%d" % c) for c in range(last)]
+        size.append(keep.tile([P, PACK, CHUNK + last], F32, name="size%d" % last))
+
+        for c in range(CHUNKS):
+            h, at = divmod(c * CHUNK, HALF)
+            words = [xg_word[h][:, z, at : at + CHUNK] for z in range(PASSES)]
+            scales = [xg_scale[z][:, c * CHUNK : (c + 1) * CHUNK] for z in range(PASSES)]
+            for z in range(PASSES):
+                nc.vector.tensor_copy(out=words[z], in_=x_word[z][:].indirect(entries(c * CHUNK, CHUNK)))
+            if c == 0:
+                idle = ppsum.tile([P, CHUNK], F32, name="p_bank")
+                for rep in range(10):
+                    nc.tensor.matmul_mx(
+                        out=idle[:],
+                        lhsT=words[0].bitcast(FP8X4),
+                        lhsT_scale=scales[0],
+                        rhs=words[0].bitcast(FP8X4),
+                        rhs_scale=scales[0],
+                        start=True,
+                        stop=True,
+                    )
+            for t in range(PACK):
+                for z in range(PASSES):
+                    nc.tensor.matmul_mx(
+                        out=z_bank[c][:, t, :],
+                        lhsT=wa[:, z, 2 * P * t : 2 * P * (t + 1)].bitcast(FP4X4),
+                        lhsT_scale=wa_scale[:, z, P * t : P * (t + 1)],
+                        rhs=words[z].bitcast(FP8X4),
+                        rhs_scale=scales[z],
+                        start=(z == 0),
+                        stop=(z == PASSES - 1),
+                    )
+            nc.scalar.activation(out=size[c][:, :, 0:CHUNK], in_=z_bank[c][:], func=ACT.Abs)
+
+        inv_factor = keep.tile([P, PACK], F32, name="inv_factor")
+        nc.vector.reciprocal(out=inv_factor[:], in_=factor[:])
+        for c in range(last):
+            nc.vector.tensor_reduce(out=size[last][:, :, CHUNK + c], in_=size[c][:], axis=AXIS.X, op=ALU.max)
+        peak = keep.tile([P, PACK], F32, name="peak")
+        nc.vector.tensor_reduce(out=peak[:], in_=size[last][:], axis=AXIS.X, op=ALU.max)
+        divisor = keep.tile([P, PACK], F32, name="divisor")
+        nc.vector.scalar_tensor_tensor(
+            out=divisor[:], in0=peak[:], scalar=0.1, in1=inv_factor[:], op0=ALU.add, op1=ALU.mult
+        )
+        gain = keep.tile([P, PACK], F32, name="gain")
+        nc.vector.reciprocal(out=gain[:], in_=divisor[:])
+
+        hid_word = keep.tile([P, J], U32, name="hid_word", align_bytes=64)
+        hid_scale = keep.tile([P, J], U8, name="hid_scale", align_bytes=64)
+
+        def quantize(hid, first, count):
+            nc.vector.quantize_mx(
+                out=hid_word[:, first : first + count].bitcast(FP8X4),
+                scales=hid_scale[:, first : first + count],
+                in_=hid[:].rearrange("p j t -> p (j t)"),
+            )
+
+        for c in range(CHUNKS // 2):
+            hid = keep.tile([P, CHUNK, PACK], BF16, name="hid%d" % c, align_bytes=64)
+            nc.vector.tensor_tensor(
+                out=hid[:],
+                in0=z_bank[c][:].rearrange("p t j -> p j t"),
+                in1=gain[:].unsqueeze(1).to_broadcast([P, CHUNK, PACK]),
+                op=ALU.mult,
+            )
+            quantize(hid, c * CHUNK, CHUNK)
+
+        def second_layer(blocks, first, count):
+            cols = slice(first, first + count)
+            p_bank = ppsum.tile([P, len(blocks), count], F32, name="p_bank")
+            for b, n in enumerate(blocks):
+                nc.tensor.matmul_mx(
+                    out=p_bank[:, b, :],
+                    lhsT=wb[:, n * P : (n + 1) * P].bitcast(FP8X4),
+                    lhsT_scale=wb_scale[:, 0, n * P : (n + 1) * P],
+                    rhs=hid_word[:, cols].bitcast(FP8X4),
+                    rhs_scale=hid_scale[:, cols],
+                    start=True,
+                    stop=True,
+                )
+            answer = stage.tile([P, len(blocks), count], F32, name="answer", tag="stage")
+            nc.scalar.copy(out=answer[:], in_=p_bank[:])
+            return answer
+
+        def place(answer, blocks, first, count):
+            for b, n in enumerate(blocks):
+                nc.vector.tensor_copy(out=placed[n % 3][:].indirect(entries(first, count)), in_=answer[:, b, :])
+
+        def finish(queue, n, first, count):
+            cols = slice(first, first + count)
+            nc.vector.scalar_tensor_tensor(
+                out=stream[n][:, cols], in0=stream[n][:, cols], scalar=0.2,
+                in1=placed[n % 3][:, cols], op0=ALU.mult, op1=ALU.add,
+            )
+            queue.dma_start(out=out[n * P : (n + 1) * P, cols], in_=stream[n][:, cols])
+
+        def finish_aside(n):
+            scaled = stage.tile([P, T], F32, name="scaled", tag="stage")
+            nc.scalar.activation(out=scaled[:], in_=stream[n][:], func=ACT.Copy, scale=0.2)
+            nc.gpsimd.tensor_tensor(out=stream[n][:], in0=scaled[:], in1=placed[n % 3][:], op=ALU.add)
+            nc.sync.dma_start(out=out[n * P : (n + 1) * P, :], in_=stream[n][:])
+
+        for c in range(CHUNKS // 2):
+            place(second_layer((0, 1), c * CHUNK, CHUNK), (0, 1), c * CHUNK, CHUNK)
+        planes = keep.tile([P, PACK, HALF], BF16, name="planes")
+        for c in range(CHUNKS // 2, CHUNKS):
+            at = c * CHUNK - HALF
+            for t in range(PACK):
+                nc.scalar.activation(
+                    out=planes[:, t, at : at + CHUNK], in_=z_bank[c][:, t, :], func=ACT.Copy, scale=gain[:, t : t + 1]
+                )
+        hid_late = keep.tile([P, HALF, PACK], BF16, name="hid_late", align_bytes=64)
+        nc.scalar.copy(
+            out=hid_late[:].rearrange("p (g i) t -> p g t i", i=4),
+            in_=planes[:].rearrange("p t (g i) -> p g t i", i=4),
+        )
+        quantize(hid_late, HALF, HALF)
+        place(second_layer((0, 1), HALF, HALF), (0, 1), HALF, HALF)
+        place(second_layer((2,), 0, J), (2,), 0, J)
+        answer_last = second_layer((3,), 0, J)
+        finish_aside(0)
+        place(answer_last, (3,), 0, J)
+        finish_aside(1)
+        finish_aside(2)
+        finish(nc.scalar, 3, 0, T // 2)
+        finish(nc.scalar, 3, T // 2, T // 2)

@@ -35,9 +35,12 @@ def tile_moe_expert_hidden_over_peak_kernel(
     with ExitStack() as ctx:
         keep = ctx.enter_context(tc.tile_pool(name="keep", bufs=1))
         reuse = ctx.enter_context(tc.tile_pool(name="reuse", bufs=1))
+        early = ctx.enter_context(tc.tile_pool(name="early", bufs=1))
+        middle = ctx.enter_context(tc.tile_pool(name="middle", bufs=1))
+        wide = ctx.enter_context(tc.tile_pool(name="wide", bufs=2))
         stage = ctx.enter_context(tc.tile_pool(name="stage", bufs=5))
         zpsum = ctx.enter_context(tc.psum_pool(name="zpsum", bufs=1))
-        ppsum = ctx.enter_context(tc.psum_pool(name="ppsum", bufs=4))
+        ppsum = ctx.enter_context(tc.psum_pool(name="ppsum", bufs=3))
 
         def entries(first, count):
             return offsets[:, first // LANES : (first + count) // LANES]
@@ -48,11 +51,10 @@ def tile_moe_expert_hidden_over_peak_kernel(
                 queue.dma_start(out=plane[i:P:QUAD].bitcast(I32), in_=rows[i])
 
         offsets = keep.tile([P, J // LANES], U16, name="offsets")
-        x_scale = keep.tile([P, T], U8, name="x_scale", align_bytes=64)
+        x_scale = early.tile([P, T], U8, name="x_scale", align_bytes=64, offset=0)
         wa_scale_raw = reuse.tile([P, PASSES, R], U8, name="wa_scale_raw", align_bytes=64, offset=0)
-        wb_scale = keep.tile([P, 1, N], U8, name="wb_scale", align_bytes=64)
         xg_scale = [keep.tile([P, J], U8, name="xg_scale%d" % z, align_bytes=64) for z in range(PASSES)]
-        for plane in (x_scale, wa_scale_raw, xg_scale[1], wb_scale):
+        for plane in (x_scale, wa_scale_raw, xg_scale[1]):
             nc.vector.memset(plane[:].bitcast(I32), 0)
 
         nc.sync.dma_start(offsets[:], offs)
@@ -61,29 +63,27 @@ def tile_moe_expert_hidden_over_peak_kernel(
                 out=x_scale[QUAD * q : QUAD * q + PASSES * ROWS, :].bitcast(I32),
                 in_=xt_scales[:, ROWS * q : ROWS * (q + 1), :].bitcast(I32),
             )
-        wa_raw = keep.tile([P, PASSES, 2 * R], U8, name="wa_raw", align_bytes=64)
+        wa_raw = middle.tile([P, PASSES, 2 * R], U8, name="wa_raw", align_bytes=64, offset=4 * T - 2 * R)
         nc.sync.dma_start(out=wa_raw[:].bitcast(I32), in_=wa_words.bitcast(I32).rearrange("z p c -> p z c"))
         x_word = []
         for z in range(PASSES):
-            x_word.append(keep.tile([P, T], U32, name="x_word%d" % z, align_bytes=64))
+            x_word.append(wide.tile([P, T], U32, name="x_word", tag="wide", align_bytes=64))
             nc.sync.dma_start(
                 out=x_word[z][:].bitcast(I32),
                 in_=xt_words[z].rearrange("p c r -> p (c r)").bitcast(I32),
             )
-        load_scale_rows(nc.scalar, wa_scale_raw, wa_scales)
+        load_scale_rows(nc.sync, wa_scale_raw, wa_scales)
 
         nc.vector.tensor_copy(out=xg_scale[0][:], in_=x_scale[:].indirect(offsets[:]))
         nc.scalar.dma_start(out=xg_scale[1][0:112, :].bitcast(I32), in_=xg_scale[0][ROWS : 112 + ROWS, :].bitcast(I32))
 
-        factor = keep.tile([P, PACK], F32, name="factor")
+        factor = early.tile([P, PACK], F32, name="factor", align_bytes=64, offset=0)
         nc.sync.dma_start(out=factor[:], in_=us.rearrange("(p t) o -> p (t o)", t=PACK))
-        wb = keep.tile([P, N], U32, name="wb", align_bytes=64)
+        wb = early.tile([P, N], U32, name="wb", align_bytes=64, offset=64 + N)
         nc.sync.dma_start(out=wb[:].bitcast(I32), in_=wb_words[0].rearrange("p c r -> p (c r)").bitcast(I32))
+        wb_scale = early.tile([P, 1, N], U8, name="wb_scale", align_bytes=64, offset=64)
+        nc.gpsimd.memset(wb_scale[:].bitcast(I32), 0)
         load_scale_rows(nc.sync, wb_scale, wb_scales)
-        stream = []
-        for n in range(N // P):
-            stream.append(keep.tile([P, T], F32, name="stream%d" % n))
-            nc.sync.dma_start(out=stream[n][:], in_=res[n * P : (n + 1) * P, :])
 
         placed = []
         for b in range(3):
@@ -100,30 +100,52 @@ def tile_moe_expert_hidden_over_peak_kernel(
             out=wa[:].bitcast(U16).rearrange("p z (t h l) -> p z h t l", t=PACK, l=8),
             in_=wa_raw[:].bitcast(U16).rearrange("p z (h l t) -> p z h t l", t=PACK, l=8),
         )
+        stream = [middle.tile([P, T], F32, name="stream%d" % n, align_bytes=64, offset=4 * T * n) for n in range(2)]
+        for n in range(2):
+            nc.sync.dma_start(out=stream[n][:], in_=res[n * P : (n + 1) * P, :])
+
+        def words(c, z):
+            h, at = divmod(c * CHUNK, HALF)
+            return xg_word[h][:, z, at : at + CHUNK]
+
+        def gather_words(c):
+            for z in range(PASSES):
+                nc.vector.tensor_copy(out=words(c, z), in_=x_word[z][:].indirect(entries(c * CHUNK, CHUNK)))
+
+        for c in range(CHUNKS // 2):
+            gather_words(c)
         nc.vector.tensor_copy(
             out=wa_scale[:].rearrange("p z (t h l) -> p z h t l", t=PACK, l=16),
             in_=wa_scale_raw[:].rearrange("p z (h l t) -> p z h t l", t=PACK, l=16),
         )
 
-        z_bank = [zpsum.tile([P, PACK, CHUNK], F32, name="z_bank%d" % c) for c in range(CHUNKS)]
+        for c in range(CHUNKS // 2, CHUNKS):
+            gather_words(c)
+        for n in range(2, 4):
+            stream.append(wide.tile([P, T], F32, name="stream", tag="wide", align_bytes=64))
+            nc.sync.dma_start(out=stream[n][:], in_=res[n * P : (n + 1) * P, :])
+
         last = CHUNKS - 1
+        z_bank = [zpsum.tile([P, PACK, CHUNK], F32, name="z_bank%d" % c) for c in range(last)]
+        z_last = [zpsum.tile([P, PACK // 2, CHUNK], F32, name="z_last%d" % u) for u in range(2)]
+
+        def sums(c, t):
+            return z_bank[c][:, t, :] if c < last else z_last[t // 2][:, t % 2, :]
+
         size = [keep.tile([P, PACK, CHUNK], F32, name="size%d" % c) for c in range(last)]
-        size.append(keep.tile([P, PACK, CHUNK + last], F32, name="size%d" % last))
+        tail = keep.tile([P, PACK, CHUNK + last], F32, name="tail")
+        size_last = [tail[:, 2 * u : 2 * u + 2, :] for u in range(2)]
 
         for c in range(CHUNKS):
-            h, at = divmod(c * CHUNK, HALF)
-            words = [xg_word[h][:, z, at : at + CHUNK] for z in range(PASSES)]
             scales = [xg_scale[z][:, c * CHUNK : (c + 1) * CHUNK] for z in range(PASSES)]
-            for z in range(PASSES):
-                nc.vector.tensor_copy(out=words[z], in_=x_word[z][:].indirect(entries(c * CHUNK, CHUNK)))
             if c == 0:
                 idle = ppsum.tile([P, CHUNK], F32, name="p_bank")
                 for rep in range(10):
                     nc.tensor.matmul_mx(
                         out=idle[:],
-                        lhsT=words[0].bitcast(FP8X4),
+                        lhsT=words(0, 0).bitcast(FP8X4),
                         lhsT_scale=scales[0],
-                        rhs=words[0].bitcast(FP8X4),
+                        rhs=words(0, 0).bitcast(FP8X4),
                         rhs_scale=scales[0],
                         start=True,
                         stop=True,
@@ -131,22 +153,27 @@ def tile_moe_expert_hidden_over_peak_kernel(
             for t in range(PACK):
                 for z in range(PASSES):
                     nc.tensor.matmul_mx(
-                        out=z_bank[c][:, t, :],
+                        out=sums(c, t),
                         lhsT=wa[:, z, 2 * P * t : 2 * P * (t + 1)].bitcast(FP4X4),
                         lhsT_scale=wa_scale[:, z, P * t : P * (t + 1)],
-                        rhs=words[z].bitcast(FP8X4),
+                        rhs=words(c, z).bitcast(FP8X4),
                         rhs_scale=scales[z],
                         start=(z == 0),
                         stop=(z == PASSES - 1),
                     )
-            nc.scalar.activation(out=size[c][:, :, 0:CHUNK], in_=z_bank[c][:], func=ACT.Abs)
+            if c < last:
+                nc.scalar.activation(out=size[c][:], in_=z_bank[c][:], func=ACT.Abs)
+            else:
+                for u in range(2):
+                    nc.scalar.activation(out=size_last[u][:, :, 0:CHUNK], in_=z_last[u][:], func=ACT.Abs)
 
         inv_factor = keep.tile([P, PACK], F32, name="inv_factor")
         nc.vector.reciprocal(out=inv_factor[:], in_=factor[:])
         for c in range(last):
-            nc.vector.tensor_reduce(out=size[last][:, :, CHUNK + c], in_=size[c][:], axis=AXIS.X, op=ALU.max)
+            nc.vector.tensor_reduce(out=tail[:, :, CHUNK + c], in_=size[c][:], axis=AXIS.X, op=ALU.max)
         peak = keep.tile([P, PACK], F32, name="peak")
-        nc.vector.tensor_reduce(out=peak[:], in_=size[last][:], axis=AXIS.X, op=ALU.max)
+        for u in range(2):
+            nc.vector.tensor_reduce(out=peak[:, 2 * u : 2 * u + 2], in_=size_last[u], axis=AXIS.X, op=ALU.max)
         divisor = keep.tile([P, PACK], F32, name="divisor")
         nc.vector.scalar_tensor_tensor(
             out=divisor[:], in0=peak[:], scalar=0.1, in1=inv_factor[:], op0=ALU.add, op1=ALU.mult
@@ -165,7 +192,7 @@ def tile_moe_expert_hidden_over_peak_kernel(
             )
 
         for c in range(CHUNKS // 2):
-            hid = keep.tile([P, CHUNK, PACK], BF16, name="hid%d" % c, align_bytes=64)
+            hid = keep.tile([P, CHUNK, PACK], BF16, name="hid", align_bytes=64)
             nc.vector.tensor_tensor(
                 out=hid[:],
                 in0=z_bank[c][:].rearrange("p t j -> p j t"),
@@ -216,7 +243,7 @@ def tile_moe_expert_hidden_over_peak_kernel(
             at = c * CHUNK - HALF
             for t in range(PACK):
                 nc.scalar.activation(
-                    out=planes[:, t, at : at + CHUNK], in_=z_bank[c][:, t, :], func=ACT.Copy, scale=gain[:, t : t + 1]
+                    out=planes[:, t, at : at + CHUNK], in_=sums(c, t), func=ACT.Copy, scale=gain[:, t : t + 1]
                 )
         hid_late = keep.tile([P, HALF, PACK], BF16, name="hid_late", align_bytes=64)
         nc.scalar.copy(

@@ -22,10 +22,14 @@ PACK = 4
 PASSES = K // (P * PACK)
 CHUNK = 128
 CHUNKS = J // CHUNK
+HALF = J // 2
 LANES = 16
 QUAD = 32
 ROWS = 4
-HALF = J // 2
+LINE = 16
+DMA_ENGINES = 16
+ALIGN = 64
+COVER = 192
 
 
 def tile_moe_expert_hidden_over_peak_kernel(
@@ -34,13 +38,13 @@ def tile_moe_expert_hidden_over_peak_kernel(
     nc = tc.nc
     with ExitStack() as ctx:
         keep = ctx.enter_context(tc.tile_pool(name="keep", bufs=1))
-        reuse = ctx.enter_context(tc.tile_pool(name="reuse", bufs=1))
-        early = ctx.enter_context(tc.tile_pool(name="early", bufs=1))
-        middle = ctx.enter_context(tc.tile_pool(name="middle", bufs=1))
-        wide = ctx.enter_context(tc.tile_pool(name="wide", bufs=2))
-        stage = ctx.enter_context(tc.tile_pool(name="stage", bufs=5))
-        zpsum = ctx.enter_context(tc.psum_pool(name="zpsum", bufs=1))
-        ppsum = ctx.enter_context(tc.psum_pool(name="ppsum", bufs=3))
+        after_wa = ctx.enter_context(tc.tile_pool(name="after_wa", bufs=1))
+        after_wa_scale = ctx.enter_context(tc.tile_pool(name="after_wa_scale", bufs=1))
+        after_x_word = ctx.enter_context(tc.tile_pool(name="after_x_word", bufs=PASSES))
+        after_planes = ctx.enter_context(tc.tile_pool(name="after_planes", bufs=1))
+        stage = ctx.enter_context(tc.tile_pool(name="stage", bufs=4))
+        z_psum = ctx.enter_context(tc.psum_pool(name="z_psum", bufs=1))
+        p_psum = ctx.enter_context(tc.psum_pool(name="p_psum", bufs=3))
 
         def entries(first, count):
             return offsets[:, first // LANES : (first + count) // LANES]
@@ -50,12 +54,20 @@ def tile_moe_expert_hidden_over_peak_kernel(
             for i in range(ROWS):
                 queue.dma_start(out=plane[i:P:QUAD].bitcast(I32), in_=rows[i])
 
+        def load_words(tile, words):
+            nc.sync.dma_start(out=tile[:].bitcast(I32), in_=words.rearrange("p c r -> p (c r)").bitcast(I32))
+
         offsets = keep.tile([P, J // LANES], U16, name="offsets")
-        x_scale = early.tile([P, T], U8, name="x_scale", align_bytes=64, offset=0)
-        wa_scale_raw = reuse.tile([P, PASSES, R], U8, name="wa_scale_raw", align_bytes=64, offset=0)
-        xg_scale = [keep.tile([P, J], U8, name="xg_scale%d" % z, align_bytes=64) for z in range(PASSES)]
+        x_scale = keep.tile([P, T], U8, name="x_scale", align_bytes=ALIGN)
+        wb_at = 0
+        wb_scale_at = wb_at + 4 * N
+        xg_late_at = wb_scale_at + N
+        wa_scale_raw = after_wa_scale.tile(
+            [P, PASSES, R], U8, name="wa_scale_raw", align_bytes=ALIGN, offset=wb_scale_at - ALIGN
+        )
+        xg_scale = [keep.tile([P, J], U8, name="xg_scale%d" % z, align_bytes=ALIGN) for z in range(PASSES)]
         for plane in (x_scale, wa_scale_raw, xg_scale[1]):
-            nc.vector.memset(plane[:].bitcast(I32), 0)
+            nc.gpsimd.memset(plane[:].bitcast(I32), 0)
 
         nc.sync.dma_start(offsets[:], offs)
         for q in range(P // QUAD):
@@ -63,117 +75,106 @@ def tile_moe_expert_hidden_over_peak_kernel(
                 out=x_scale[QUAD * q : QUAD * q + PASSES * ROWS, :].bitcast(I32),
                 in_=xt_scales[:, ROWS * q : ROWS * (q + 1), :].bitcast(I32),
             )
-        wa_raw = middle.tile([P, PASSES, 2 * R], U8, name="wa_raw", align_bytes=64, offset=4 * T - 2 * R)
+        wa_raw = keep.tile([P, PASSES, 2 * R], U8, name="wa_raw", align_bytes=ALIGN)
         nc.sync.dma_start(out=wa_raw[:].bitcast(I32), in_=wa_words.bitcast(I32).rearrange("z p c -> p z c"))
-        x_word = []
+        x_word = [after_x_word.tile([P, T], U32, name="x_word", tag="wide", align_bytes=ALIGN) for z in range(PASSES)]
         for z in range(PASSES):
-            x_word.append(wide.tile([P, T], U32, name="x_word", tag="wide", align_bytes=64))
-            nc.sync.dma_start(
-                out=x_word[z][:].bitcast(I32),
-                in_=xt_words[z].rearrange("p c r -> p (c r)").bitcast(I32),
-            )
+            load_words(x_word[z], xt_words[z])
         load_scale_rows(nc.sync, wa_scale_raw, wa_scales)
+        factor = keep.tile([P, PACK], F32, name="factor")
+        nc.sync.dma_start(out=factor[:], in_=us.rearrange("(p t) o -> p (t o)", t=PACK))
 
         nc.vector.tensor_copy(out=xg_scale[0][:], in_=x_scale[:].indirect(offsets[:]))
-        nc.scalar.dma_start(out=xg_scale[1][0:112, :].bitcast(I32), in_=xg_scale[0][ROWS : 112 + ROWS, :].bitcast(I32))
+        moved = P - DMA_ENGINES
+        nc.scalar.dma_start(
+            out=xg_scale[1][0:moved, :].bitcast(I32), in_=xg_scale[0][ROWS : moved + ROWS, :].bitcast(I32)
+        )
 
-        factor = early.tile([P, PACK], F32, name="factor", align_bytes=64, offset=0)
-        nc.sync.dma_start(out=factor[:], in_=us.rearrange("(p t) o -> p (t o)", t=PACK))
-        wb = early.tile([P, N], U32, name="wb", align_bytes=64, offset=64 + N)
-        nc.sync.dma_start(out=wb[:].bitcast(I32), in_=wb_words[0].rearrange("p c r -> p (c r)").bitcast(I32))
-        wb_scale = early.tile([P, 1, N], U8, name="wb_scale", align_bytes=64, offset=64)
+        windows = 3
+        placed = [keep.tile([P, T], F32, name="placed%d" % b) for b in range(windows)]
+        for window in placed:
+            nc.gpsimd.memset(window[:].bitcast(I32), 0)
+
+        wa = after_wa.tile([P, PASSES, 2 * R], U8, name="wa", align_bytes=ALIGN, offset=4 * T - 2 * R)
+        wa_scale = keep.tile([P, PASSES, R], U8, name="wa_scale", align_bytes=ALIGN)
+
+        def permute_columns(target, source, run):
+            nc.vector.tensor_copy(
+                out=target.rearrange("p z (t h l) -> p z h t l", t=PACK, l=run),
+                in_=source.rearrange("p z (h l t) -> p z h t l", t=PACK, l=run),
+            )
+
+        permute_columns(wa[:].bitcast(U16), wa_raw[:].bitcast(U16), LINE // 2)
+
+        xg_first = keep.tile([P, J], U32, name="xg_first", align_bytes=ALIGN)
+        xg_second = keep.tile([P, CHUNK], U32, name="xg_second", align_bytes=ALIGN)
+        xg_late = after_wa_scale.tile([P, J - CHUNK], U32, name="xg_late", align_bytes=ALIGN, offset=xg_late_at)
+
+        def gathered(z, first, count):
+            if z == 0:
+                return xg_first[:, first : first + count]
+            if first < CHUNK:
+                return xg_second[:, first : first + count]
+            return xg_late[:, first - CHUNK : first - CHUNK + count]
+
+        def gather_words(z, first, count):
+            nc.vector.tensor_copy(out=gathered(z, first, count), in_=x_word[z][:].indirect(entries(first, count)))
+
+        gather_words(0, 0, J)
+        permute_columns(wa_scale[:], wa_scale_raw[:], LINE)
+        for first in range(0, J, CHUNK):
+            gather_words(1, first, CHUNK)
+
+        wb = after_wa_scale.tile([P, N], U32, name="wb", align_bytes=ALIGN, offset=wb_at)
+        load_words(wb, wb_words[0])
+        wb_scale = after_wa_scale.tile([P, 1, N], U8, name="wb_scale", align_bytes=ALIGN, offset=wb_scale_at)
         nc.gpsimd.memset(wb_scale[:].bitcast(I32), 0)
         load_scale_rows(nc.sync, wb_scale, wb_scales)
+        stream = []
 
-        placed = []
-        for b in range(3):
-            placed.append(keep.tile([P, T], F32, name="placed%d" % b))
-            nc.vector.memset(placed[b][:].bitcast(I32), 0)
+        def load_residual(tile):
+            n = len(stream)
+            stream.append(tile)
+            nc.sync.dma_start(out=tile[:], in_=res[n * P : (n + 1) * P, :])
 
-        xg_word = [
-            keep.tile([P, PASSES, HALF], U32, name="xg_word0", align_bytes=64),
-            reuse.tile([P, PASSES, HALF], U32, name="xg_word1", align_bytes=64, offset=0),
-        ]
-        wa = keep.tile([P, PASSES, 2 * R], U8, name="wa", align_bytes=64)
-        wa_scale = keep.tile([P, PASSES, R], U8, name="wa_scale", align_bytes=64)
-        nc.vector.tensor_copy(
-            out=wa[:].bitcast(U16).rearrange("p z (t h l) -> p z h t l", t=PACK, l=8),
-            in_=wa_raw[:].bitcast(U16).rearrange("p z (h l t) -> p z h t l", t=PACK, l=8),
-        )
-        stream = [middle.tile([P, T], F32, name="stream%d" % n, align_bytes=64, offset=4 * T * n) for n in range(2)]
-        for n in range(2):
-            nc.sync.dma_start(out=stream[n][:], in_=res[n * P : (n + 1) * P, :])
-
-        def words(c, z):
-            h, at = divmod(c * CHUNK, HALF)
-            return xg_word[h][:, z, at : at + CHUNK]
-
-        def gather_words(c):
-            for z in range(PASSES):
-                nc.vector.tensor_copy(out=words(c, z), in_=x_word[z][:].indirect(entries(c * CHUNK, CHUNK)))
-
-        for c in range(CHUNKS // 2):
-            gather_words(c)
-        nc.vector.tensor_copy(
-            out=wa_scale[:].rearrange("p z (t h l) -> p z h t l", t=PACK, l=16),
-            in_=wa_scale_raw[:].rearrange("p z (h l t) -> p z h t l", t=PACK, l=16),
-        )
-
-        for c in range(CHUNKS // 2, CHUNKS):
-            gather_words(c)
-        for n in range(2, 4):
-            stream.append(wide.tile([P, T], F32, name="stream", tag="wide", align_bytes=64))
-            nc.sync.dma_start(out=stream[n][:], in_=res[n * P : (n + 1) * P, :])
+        for z in range(PASSES):
+            load_residual(after_x_word.tile([P, T], F32, name="stream", tag="wide", align_bytes=ALIGN))
 
         last = CHUNKS - 1
-        z_bank = [zpsum.tile([P, PACK, CHUNK], F32, name="z_bank%d" % c) for c in range(last)]
-        z_last = [zpsum.tile([P, PACK // 2, CHUNK], F32, name="z_last%d" % u) for u in range(2)]
+        z_bank = [z_psum.tile([P, PACK, CHUNK], F32, name="z_bank%d" % c) for c in range(last)]
+        z_last = [z_psum.tile([P, 2, CHUNK], F32, name="z_last%d" % u) for u in range(PACK // 2)]
 
         def sums(c, t):
             return z_bank[c][:, t, :] if c < last else z_last[t // 2][:, t % 2, :]
 
         size = [keep.tile([P, PACK, CHUNK], F32, name="size%d" % c) for c in range(last)]
-        tail = keep.tile([P, PACK, CHUNK + last], F32, name="tail")
-        size_last = [tail[:, 2 * u : 2 * u + 2, :] for u in range(2)]
-
+        size_last = keep.tile([P, PACK, CHUNK + last], F32, name="size_last")
         for c in range(CHUNKS):
-            scales = [xg_scale[z][:, c * CHUNK : (c + 1) * CHUNK] for z in range(PASSES)]
-            if c == 0:
-                idle = ppsum.tile([P, CHUNK], F32, name="p_bank")
-                for rep in range(10):
-                    nc.tensor.matmul_mx(
-                        out=idle[:],
-                        lhsT=words(0, 0).bitcast(FP8X4),
-                        lhsT_scale=scales[0],
-                        rhs=words(0, 0).bitcast(FP8X4),
-                        rhs_scale=scales[0],
-                        start=True,
-                        stop=True,
-                    )
             for t in range(PACK):
                 for z in range(PASSES):
                     nc.tensor.matmul_mx(
                         out=sums(c, t),
                         lhsT=wa[:, z, 2 * P * t : 2 * P * (t + 1)].bitcast(FP4X4),
                         lhsT_scale=wa_scale[:, z, P * t : P * (t + 1)],
-                        rhs=words(c, z).bitcast(FP8X4),
-                        rhs_scale=scales[z],
+                        rhs=gathered(z, c * CHUNK, CHUNK).bitcast(FP8X4),
+                        rhs_scale=xg_scale[z][:, c * CHUNK : (c + 1) * CHUNK],
                         start=(z == 0),
                         stop=(z == PASSES - 1),
                     )
             if c < last:
                 nc.scalar.activation(out=size[c][:], in_=z_bank[c][:], func=ACT.Abs)
-            else:
-                for u in range(2):
-                    nc.scalar.activation(out=size_last[u][:, :, 0:CHUNK], in_=z_last[u][:], func=ACT.Abs)
+        for u in range(PACK // 2):
+            nc.scalar.activation(out=size_last[:, 2 * u : 2 * u + 2, 0:CHUNK], in_=z_last[u][:], func=ACT.Abs)
+
+        for b in range(2):
+            load_residual(after_wa.tile([P, T], F32, name="stream%d" % b, align_bytes=ALIGN, offset=4 * T * b))
 
         inv_factor = keep.tile([P, PACK], F32, name="inv_factor")
         nc.vector.reciprocal(out=inv_factor[:], in_=factor[:])
         for c in range(last):
-            nc.vector.tensor_reduce(out=tail[:, :, CHUNK + c], in_=size[c][:], axis=AXIS.X, op=ALU.max)
+            nc.vector.tensor_reduce(out=size_last[:, :, CHUNK + c], in_=size[c][:], axis=AXIS.X, op=ALU.max)
         peak = keep.tile([P, PACK], F32, name="peak")
-        for u in range(2):
-            nc.vector.tensor_reduce(out=peak[:, 2 * u : 2 * u + 2], in_=size_last[u], axis=AXIS.X, op=ALU.max)
+        nc.vector.tensor_reduce(out=peak[:], in_=size_last[:], axis=AXIS.X, op=ALU.max)
         divisor = keep.tile([P, PACK], F32, name="divisor")
         nc.vector.scalar_tensor_tensor(
             out=divisor[:], in0=peak[:], scalar=0.1, in1=inv_factor[:], op0=ALU.add, op1=ALU.mult
@@ -181,8 +182,8 @@ def tile_moe_expert_hidden_over_peak_kernel(
         gain = keep.tile([P, PACK], F32, name="gain")
         nc.vector.reciprocal(out=gain[:], in_=divisor[:])
 
-        hid_word = keep.tile([P, J], U32, name="hid_word", align_bytes=64)
-        hid_scale = keep.tile([P, J], U8, name="hid_scale", align_bytes=64)
+        hid_word = keep.tile([P, J], U32, name="hid_word", align_bytes=ALIGN)
+        hid_scale = keep.tile([P, J], U8, name="hid_scale", align_bytes=ALIGN)
 
         def quantize(hid, first, count):
             nc.vector.quantize_mx(
@@ -191,19 +192,9 @@ def tile_moe_expert_hidden_over_peak_kernel(
                 in_=hid[:].rearrange("p j t -> p (j t)"),
             )
 
-        for c in range(CHUNKS // 2):
-            hid = keep.tile([P, CHUNK, PACK], BF16, name="hid", align_bytes=64)
-            nc.vector.tensor_tensor(
-                out=hid[:],
-                in0=z_bank[c][:].rearrange("p t j -> p j t"),
-                in1=gain[:].unsqueeze(1).to_broadcast([P, CHUNK, PACK]),
-                op=ALU.mult,
-            )
-            quantize(hid, c * CHUNK, CHUNK)
-
-        def second_layer(blocks, first, count):
+        def second_product(answer, blocks, first, count):
             cols = slice(first, first + count)
-            p_bank = ppsum.tile([P, len(blocks), count], F32, name="p_bank")
+            p_bank = p_psum.tile([P, len(blocks), count], F32, name="p_bank")
             for b, n in enumerate(blocks):
                 nc.tensor.matmul_mx(
                     out=p_bank[:, b, :],
@@ -214,49 +205,74 @@ def tile_moe_expert_hidden_over_peak_kernel(
                     start=True,
                     stop=True,
                 )
+            nc.scalar.copy(out=answer, in_=p_bank[:])
+
+        def scatter(values, n, first, count):
+            nc.vector.tensor_copy(out=placed[n % windows][:].indirect(entries(first, count)), in_=values)
+
+        def multiply_and_scatter(blocks, first, count):
             answer = stage.tile([P, len(blocks), count], F32, name="answer", tag="stage")
-            nc.scalar.copy(out=answer[:], in_=p_bank[:])
-            return answer
-
-        def place(answer, blocks, first, count):
+            second_product(answer[:], blocks, first, count)
             for b, n in enumerate(blocks):
-                nc.vector.tensor_copy(out=placed[n % 3][:].indirect(entries(first, count)), in_=answer[:, b, :])
-
-        def finish(queue, n, first, count):
-            cols = slice(first, first + count)
-            nc.vector.scalar_tensor_tensor(
-                out=stream[n][:, cols], in0=stream[n][:, cols], scalar=0.2,
-                in1=placed[n % 3][:, cols], op0=ALU.mult, op1=ALU.add,
-            )
-            queue.dma_start(out=out[n * P : (n + 1) * P, cols], in_=stream[n][:, cols])
-
-        def finish_aside(n):
-            scaled = stage.tile([P, T], F32, name="scaled", tag="stage")
-            nc.scalar.activation(out=scaled[:], in_=stream[n][:], func=ACT.Copy, scale=0.2)
-            nc.gpsimd.tensor_tensor(out=stream[n][:], in0=scaled[:], in1=placed[n % 3][:], op=ALU.add)
-            nc.sync.dma_start(out=out[n * P : (n + 1) * P, :], in_=stream[n][:])
+                scatter(answer[:, b, :], n, first, count)
 
         for c in range(CHUNKS // 2):
-            place(second_layer((0, 1), c * CHUNK, CHUNK), (0, 1), c * CHUNK, CHUNK)
-        planes = keep.tile([P, PACK, HALF], BF16, name="planes")
+            hid_early = keep.tile([P, CHUNK, PACK], BF16, name="hid_early", align_bytes=ALIGN)
+            nc.vector.tensor_tensor(
+                out=hid_early[:],
+                in0=z_bank[c][:].rearrange("p t j -> p j t"),
+                in1=gain[:].unsqueeze(1).to_broadcast([P, CHUNK, PACK]),
+                op=ALU.mult,
+            )
+            quantize(hid_early, c * CHUNK, CHUNK)
+        for c in range(CHUNKS // 2):
+            multiply_and_scatter((0, 1), c * CHUNK, CHUNK)
+
+        hid_by_t = after_planes.tile([P, PACK, HALF], BF16, name="hid_by_t", offset=0)
         for c in range(CHUNKS // 2, CHUNKS):
             at = c * CHUNK - HALF
             for t in range(PACK):
                 nc.scalar.activation(
-                    out=planes[:, t, at : at + CHUNK], in_=sums(c, t), func=ACT.Copy, scale=gain[:, t : t + 1]
+                    out=hid_by_t[:, t, at : at + CHUNK], in_=sums(c, t), func=ACT.Copy, scale=gain[:, t : t + 1]
                 )
-        hid_late = keep.tile([P, HALF, PACK], BF16, name="hid_late", align_bytes=64)
+        hid_late = keep.tile([P, HALF, PACK], BF16, name="hid_late", align_bytes=ALIGN)
         nc.scalar.copy(
             out=hid_late[:].rearrange("p (g i) t -> p g t i", i=4),
-            in_=planes[:].rearrange("p t (g i) -> p g t i", i=4),
+            in_=hid_by_t[:].rearrange("p t (g i) -> p g t i", i=4),
         )
         quantize(hid_late, HALF, HALF)
-        place(second_layer((0, 1), HALF, HALF), (0, 1), HALF, HALF)
-        place(second_layer((2,), 0, J), (2,), 0, J)
-        answer_last = second_layer((3,), 0, J)
-        finish_aside(0)
-        place(answer_last, (3,), 0, J)
-        finish_aside(1)
-        finish_aside(2)
-        finish(nc.scalar, 3, 0, T // 2)
-        finish(nc.scalar, 3, T // 2, T // 2)
+
+        answer2 = after_planes.tile([P, 1, J], F32, name="answer2", offset=0)
+        second_product(answer2[:, :, 0:HALF], (2,), 0, HALF)
+        scatter(answer2[:, 0, 0:COVER], 2, 0, COVER)
+        multiply_and_scatter((0, 1), HALF, HALF)
+        second_product(answer2[:, :, HALF:J], (2,), HALF, HALF)
+        scatter(answer2[:, 0, COVER:J], 2, COVER, J - COVER)
+        answer3 = stage.tile([P, 1, J], F32, name="answer", tag="stage")
+        second_product(answer3[:], (3,), 0, J)
+
+        whole = [slice(0, T)]
+        halves = [slice(first, first + T // 2) for first in range(0, T, T // 2)]
+
+        def finish_aside(n, pieces):
+            scaled = stage.tile([P, T], F32, name="scaled", tag="stage")
+            nc.scalar.activation(out=scaled[:], in_=stream[n][:], func=ACT.Copy, scale=0.2)
+            for cols in pieces:
+                nc.gpsimd.tensor_tensor(out=stream[n][:, cols], in0=scaled[:, cols], in1=placed[n][:, cols], op=ALU.add)
+                nc.sync.dma_start(out=out[n * P : (n + 1) * P, cols], in_=stream[n][:, cols])
+
+        finish_aside(0, whole)
+        scatter(answer3[:, 0, :], 3, 0, J)
+        finish_aside(1, whole)
+        finish_aside(2, halves)
+
+        for cols in halves:
+            nc.vector.scalar_tensor_tensor(
+                out=stream[3][:, cols],
+                in0=stream[3][:, cols],
+                scalar=0.2,
+                in1=placed[3 % windows][:, cols],
+                op0=ALU.mult,
+                op1=ALU.add,
+            )
+            nc.scalar.dma_start(out=out[3 * P : 4 * P, cols], in_=stream[3][:, cols])

from contextlib import ExitStack

import concourse.mybir as mybir

K, T, J, R, N = 1024, 1024, 512, 512, 512
FLOPS = 2 * K * R * J + 2 * R * N * J

F32 = mybir.dt.float32
BF16 = mybir.dt.bfloat16
I32 = mybir.dt.int32
U32 = mybir.dt.uint32
U16 = mybir.dt.uint16
U8 = mybir.dt.uint8
FP8X4 = mybir.dt.float8_e4m3fn_x4
FP4X4 = mybir.dt.float4_e2m1fn_x4
ALU = mybir.AluOpType
ACT = mybir.ActivationFunctionType
AXIS = mybir.AxisListType

P = 128
PACK = 4
PASSES = K // (P * PACK)
CHUNK = 128
CHUNKS = J // CHUNK
HALF = J // 2
LANES = 16
QUAD = 32
ROWS = 4
LINE = 16
DMA_ENGINES = 16
ALIGN = 64
COVER = 192


def tile_moe_expert_hidden_over_peak_kernel(
    tc, xt_words, xt_scales, wa_words, wa_scales, us, wb_words, wb_scales, res, offs, out
):
    nc = tc.nc
    with ExitStack() as ctx:
        keep = ctx.enter_context(tc.tile_pool(name="keep", bufs=1))
        after_wa = ctx.enter_context(tc.tile_pool(name="after_wa", bufs=1))
        after_wa_scale = ctx.enter_context(tc.tile_pool(name="after_wa_scale", bufs=1))
        after_x_word = ctx.enter_context(tc.tile_pool(name="after_x_word", bufs=PASSES))
        after_planes = ctx.enter_context(tc.tile_pool(name="after_planes", bufs=1))
        stage = ctx.enter_context(tc.tile_pool(name="stage", bufs=4))
        z_psum = ctx.enter_context(tc.psum_pool(name="z_psum", bufs=1))
        p_psum = ctx.enter_context(tc.psum_pool(name="p_psum", bufs=3))

        def entries(first, count):
            return offsets[:, first // LANES : (first + count) // LANES]

        def load_scale_rows(queue, plane, scales):
            rows = scales.bitcast(I32).rearrange("z (q i) c -> i q z c", i=ROWS)
            for i in range(ROWS):
                queue.dma_start(out=plane[i:P:QUAD].bitcast(I32), in_=rows[i])

        def load_words(tile, words):
            nc.sync.dma_start(out=tile[:].bitcast(I32), in_=words.rearrange("p c r -> p (c r)").bitcast(I32))

        offsets = keep.tile([P, J // LANES], U16, name="offsets")
        x_scale = keep.tile([P, T], U8, name="x_scale", align_bytes=ALIGN)
        wb_at = 0
        wb_scale_at = wb_at + 4 * N
        xg_late_at = wb_scale_at + N
        wa_scale_raw = after_wa_scale.tile(
            [P, PASSES, R], U8, name="wa_scale_raw", align_bytes=ALIGN, offset=wb_scale_at - ALIGN
        )
        xg_scale = [keep.tile([P, J], U8, name="xg_scale%d" % z, align_bytes=ALIGN) for z in range(PASSES)]
        for plane in (x_scale, wa_scale_raw, xg_scale[1]):
            nc.gpsimd.memset(plane[:].bitcast(I32), 0)

        nc.sync.dma_start(offsets[:], offs)
        for q in range(P // QUAD):
            nc.sync.dma_start(
                out=x_scale[QUAD * q : QUAD * q + PASSES * ROWS, :].bitcast(I32),
                in_=xt_scales[:, ROWS * q : ROWS * (q + 1), :].bitcast(I32),
            )
        wa_raw = keep.tile([P, PASSES, 2 * R], U8, name="wa_raw", align_bytes=ALIGN)
        nc.sync.dma_start(out=wa_raw[:].bitcast(I32), in_=wa_words.bitcast(I32).rearrange("z p c -> p z c"))
        x_word = [after_x_word.tile([P, T], U32, name="x_word", tag="wide", align_bytes=ALIGN) for z in range(PASSES)]
        for z in range(PASSES):
            load_words(x_word[z], xt_words[z])
        load_scale_rows(nc.sync, wa_scale_raw, wa_scales)
        factor = keep.tile([P, PACK], F32, name="factor")
        nc.sync.dma_start(out=factor[:], in_=us.rearrange("(p t) o -> p (t o)", t=PACK))

        nc.vector.tensor_copy(out=xg_scale[0][:], in_=x_scale[:].indirect(offsets[:]))
        moved = P - DMA_ENGINES
        nc.scalar.dma_start(
            out=xg_scale[1][0:moved, :].bitcast(I32), in_=xg_scale[0][ROWS : moved + ROWS, :].bitcast(I32)
        )

        windows = 3
        placed = [keep.tile([P, T], F32, name="placed%d" % b) for b in range(windows)]
        for window in placed:
            nc.gpsimd.memset(window[:].bitcast(I32), 0)

        wa = after_wa.tile([P, PASSES, 2 * R], U8, name="wa", align_bytes=ALIGN, offset=4 * T - 2 * R)
        wa_scale = keep.tile([P, PASSES, R], U8, name="wa_scale", align_bytes=ALIGN)

        def permute_columns(target, source, run):
            nc.vector.tensor_copy(
                out=target.rearrange("p z (t h l) -> p z h t l", t=PACK, l=run),
                in_=source.rearrange("p z (h l t) -> p z h t l", t=PACK, l=run),
            )

        permute_columns(wa[:].bitcast(U16), wa_raw[:].bitcast(U16), LINE // 2)

        xg_first = keep.tile([P, J], U32, name="xg_first", align_bytes=ALIGN)
        xg_second = keep.tile([P, CHUNK], U32, name="xg_second", align_bytes=ALIGN)
        xg_late = after_wa_scale.tile([P, J - CHUNK], U32, name="xg_late", align_bytes=ALIGN, offset=xg_late_at)

        def gathered(z, first, count):
            if z == 0:
                return xg_first[:, first : first + count]
            if first < CHUNK:
                return xg_second[:, first : first + count]
            return xg_late[:, first - CHUNK : first - CHUNK + count]

        def gather_words(z, first, count):
            nc.vector.tensor_copy(out=gathered(z, first, count), in_=x_word[z][:].indirect(entries(first, count)))

        gather_words(0, 0, J)
        permute_columns(wa_scale[:], wa_scale_raw[:], LINE)
        for first in range(0, J, CHUNK):
            gather_words(1, first, CHUNK)

        wb = after_wa_scale.tile([P, N], U32, name="wb", align_bytes=ALIGN, offset=wb_at)
        load_words(wb, wb_words[0])
        wb_scale = after_wa_scale.tile([P, 1, N], U8, name="wb_scale", align_bytes=ALIGN, offset=wb_scale_at)
        nc.gpsimd.memset(wb_scale[:].bitcast(I32), 0)
        load_scale_rows(nc.sync, wb_scale, wb_scales)
        stream = []

        def load_residual(tile):
            n = len(stream)
            stream.append(tile)
            nc.sync.dma_start(out=tile[:], in_=res[n * P : (n + 1) * P, :])

        for z in range(PASSES):
            load_residual(after_x_word.tile([P, T], F32, name="stream", tag="wide", align_bytes=ALIGN))

        last = CHUNKS - 1
        z_bank = [z_psum.tile([P, PACK, CHUNK], F32, name="z_bank%d" % c) for c in range(last)]
        z_last = [z_psum.tile([P, 2, CHUNK], F32, name="z_last%d" % u) for u in range(PACK // 2)]

        def sums(c, t):
            return z_bank[c][:, t, :] if c < last else z_last[t // 2][:, t % 2, :]

        size = [keep.tile([P, PACK, CHUNK], F32, name="size%d" % c) for c in range(last)]
        size_last = keep.tile([P, PACK, CHUNK + last], F32, name="size_last")
        for c in range(CHUNKS):
            for t in range(PACK):
                for z in range(PASSES):
                    nc.tensor.matmul_mx(
                        out=sums(c, t),
                        lhsT=wa[:, z, 2 * P * t : 2 * P * (t + 1)].bitcast(FP4X4),
                        lhsT_scale=wa_scale[:, z, P * t : P * (t + 1)],
                        rhs=gathered(z, c * CHUNK, CHUNK).bitcast(FP8X4),
                        rhs_scale=xg_scale[z][:, c * CHUNK : (c + 1) * CHUNK],
                        start=(z == 0),
                        stop=(z == PASSES - 1),
                    )
            if c < last:
                nc.scalar.activation(out=size[c][:], in_=z_bank[c][:], func=ACT.Abs)
        for u in range(PACK // 2):
            nc.scalar.activation(out=size_last[:, 2 * u : 2 * u + 2, 0:CHUNK], in_=z_last[u][:], func=ACT.Abs)

        for b in range(2):
            load_residual(after_wa.tile([P, T], F32, name="stream%d" % b, align_bytes=ALIGN, offset=4 * T * b))

        inv_factor = keep.tile([P, PACK], F32, name="inv_factor")
        nc.vector.reciprocal(out=inv_factor[:], in_=factor[:])
        for c in range(last):
            nc.vector.tensor_reduce(out=size_last[:, :, CHUNK + c], in_=size[c][:], axis=AXIS.X, op=ALU.max)
        peak = keep.tile([P, PACK], F32, name="peak")
        nc.vector.tensor_reduce(out=peak[:], in_=size_last[:], axis=AXIS.X, op=ALU.max)
        divisor = keep.tile([P, PACK], F32, name="divisor")
        nc.vector.scalar_tensor_tensor(
            out=divisor[:], in0=peak[:], scalar=0.1, in1=inv_factor[:], op0=ALU.add, op1=ALU.mult
        )
        gain = keep.tile([P, PACK], F32, name="gain")
        nc.vector.reciprocal(out=gain[:], in_=divisor[:])

        hid_word = keep.tile([P, J], U32, name="hid_word", align_bytes=ALIGN)
        hid_scale = keep.tile([P, J], U8, name="hid_scale", align_bytes=ALIGN)

        def quantize(hid, first, count):
            nc.vector.quantize_mx(
                out=hid_word[:, first : first + count].bitcast(FP8X4),
                scales=hid_scale[:, first : first + count],
                in_=hid[:].rearrange("p j t -> p (j t)"),
            )

        def second_product(answer, blocks, first, count):
            cols = slice(first, first + count)
            p_bank = p_psum.tile([P, len(blocks), count], F32, name="p_bank")
            for b, n in enumerate(blocks):
                nc.tensor.matmul_mx(
                    out=p_bank[:, b, :],
                    lhsT=wb[:, n * P : (n + 1) * P].bitcast(FP8X4),
                    lhsT_scale=wb_scale[:, 0, n * P : (n + 1) * P],
                    rhs=hid_word[:, cols].bitcast(FP8X4),
                    rhs_scale=hid_scale[:, cols],
                    start=True,
                    stop=True,
                )
            nc.scalar.copy(out=answer, in_=p_bank[:])

        def scatter(values, n, first, count):
            nc.vector.tensor_copy(out=placed[n % windows][:].indirect(entries(first, count)), in_=values)

        def multiply_and_scatter(blocks, first, count):
            answer = stage.tile([P, len(blocks), count], F32, name="answer", tag="stage")
            second_product(answer[:], blocks, first, count)
            for b, n in enumerate(blocks):
                scatter(answer[:, b, :], n, first, count)

        for c in range(CHUNKS // 2):
            hid_early = keep.tile([P, CHUNK, PACK], BF16, name="hid_early", align_bytes=ALIGN)
            nc.vector.tensor_tensor(
                out=hid_early[:],
                in0=z_bank[c][:].rearrange("p t j -> p j t"),
                in1=gain[:].unsqueeze(1).to_broadcast([P, CHUNK, PACK]),
                op=ALU.mult,
            )
            quantize(hid_early, c * CHUNK, CHUNK)
        for c in range(CHUNKS // 2):
            multiply_and_scatter((0, 1), c * CHUNK, CHUNK)

        hid_by_t = after_planes.tile([P, PACK, HALF], BF16, name="hid_by_t", offset=0)
        for c in range(CHUNKS // 2, CHUNKS):
            at = c * CHUNK - HALF
            for t in range(PACK):
                nc.scalar.activation(
                    out=hid_by_t[:, t, at : at + CHUNK], in_=sums(c, t), func=ACT.Copy, scale=gain[:, t : t + 1]
                )
        hid_late = keep.tile([P, HALF, PACK], BF16, name="hid_late", align_bytes=ALIGN)
        nc.scalar.copy(
            out=hid_late[:].rearrange("p (g i) t -> p g t i", i=4),
            in_=hid_by_t[:].rearrange("p t (g i) -> p g t i", i=4),
        )
        quantize(hid_late, HALF, HALF)

        answer2 = after_planes.tile([P, 1, J], F32, name="answer2", offset=0)
        second_product(answer2[:, :, 0:HALF], (2,), 0, HALF)
        scatter(answer2[:, 0, 0:COVER], 2, 0, COVER)
        multiply_and_scatter((0, 1), HALF, HALF)
        second_product(answer2[:, :, HALF:J], (2,), HALF, HALF)
        scatter(answer2[:, 0, COVER:J], 2, COVER, J - COVER)
        answer3 = stage.tile([P, 1, J], F32, name="answer", tag="stage")
        second_product(answer3[:], (3,), 0, J)

        whole = [slice(0, T)]
        halves = [slice(first, first + T // 2) for first in range(0, T, T // 2)]

        def finish_aside(n, pieces):
            scaled = stage.tile([P, T], F32, name="scaled", tag="stage")
            nc.scalar.activation(out=scaled[:], in_=stream[n][:], func=ACT.Copy, scale=0.2)
            for cols in pieces:
                nc.gpsimd.tensor_tensor(out=stream[n][:, cols], in0=scaled[:, cols], in1=placed[n][:, cols], op=ALU.add)
                nc.sync.dma_start(out=out[n * P : (n + 1) * P, cols], in_=stream[n][:, cols])

        finish_aside(0, whole)
        scatter(answer3[:, 0, :], 3, 0, J)
        finish_aside(1, whole)
        finish_aside(2, halves)

        for cols in halves:
            nc.vector.scalar_tensor_tensor(
                out=stream[3][:, cols],
                in0=stream[3][:, cols],
                scalar=0.2,
                in1=placed[3 % windows][:, cols],
                op0=ALU.mult,
                op1=ALU.add,
            )
            nc.scalar.dma_start(out=out[3 * P : 4 * P, cols], in_=stream[3][:, cols])
